import numpy as np
import ml_dtypes


def mxq(x, axis, fmt="e4m3"):
    dtype, down = {"e4m3": (ml_dtypes.float8_e4m3fn, 7), "e5m2": (ml_dtypes.float8_e5m2, 14)}[fmt]
    v = np.moveaxis(np.asarray(x, np.float32).astype(ml_dtypes.bfloat16).astype(np.float64), axis, -1)
    blocks = v.reshape(v.shape[:-1] + (-1, 32))
    amax = np.abs(blocks).max(-1, keepdims=True)
    byte = np.maximum(np.where(amax > 0, np.frexp(amax)[1] - 1 + 127, 0) - down, 1)
    scale = np.exp2(byte - 127.0)
    codes = (blocks / scale).astype(np.float32).astype(dtype).astype(np.float64)
    return np.moveaxis((codes * scale).reshape(v.shape), -1, axis)


WIDE = False


def mx_kscale(k):
    if not WIDE:
        return np.ones(k)
    levels = np.array([10, -10, 5, -5, 0])
    if k % 512:
        return np.exp2(np.random.permutation(np.resize(levels, k // 32))).repeat(32)
    a = np.empty((k // 512, 16))
    for p in range(k // 512):
        a[p, :8] = np.random.permutation(np.resize(levels, 8))
        for g in range(8):
            far = levels[np.abs(levels - a[p, g]) >= 10]
            a[p, g + 8] = far[np.random.randint(len(far))]
    return np.exp2(a.ravel()).repeat(32)


def f64(x):
    return np.asarray(x).astype(np.float64)


E2M1 = np.array([0.0, 0.5, 1.0, 1.5, 2.0, 3.0, 4.0, 6.0, -0.0, -0.5, -1.0, -1.5, -2.0, -3.0, -4.0, -6.0])


def pack_weight(w, fmt):
    k, n = w.shape
    w = f64(np.asarray(w, np.float32).astype(ml_dtypes.bfloat16)).reshape(k // 32, 32, n)
    amax = np.abs(w).max(1)
    if fmt == "e4m3":
        byte = np.frexp(amax)[1] - 1 + 127 - 7
    else:
        mant, ex = np.frexp(amax / 6.0)
        byte = np.where(mant > 0.5, ex, ex - 1) + 127
    byte = np.clip(np.where(amax > 0, byte, 1), 1, 254)
    scaled = (w * np.exp2(127.0 - byte)[:, None, :]).reshape(k, n).astype(np.float32)
    by_word = np.ascontiguousarray(scaled.reshape(k // 512, 128, 4, n).transpose(0, 1, 3, 2))
    if fmt == "e4m3":
        words = by_word.astype(ml_dtypes.float8_e4m3fn).view(np.uint8)
    else:
        c = by_word.astype(ml_dtypes.float4_e2m1fn).view(np.uint8) & 0xF
        words = (c[..., 0::2] | (c[..., 1::2] << 4)).reshape(k // 512, 128, 2 * n)
    return np.ascontiguousarray(words), np.ascontiguousarray(byte.astype(np.uint8).reshape(k // 512, 16, n))


def unpack_weight(words, scales, fmt):
    g, _, n = scales.shape
    words = np.ascontiguousarray(words).reshape(g, 128, n, -1)
    if fmt == "e4m3":
        vals = words.view(ml_dtypes.float8_e4m3fn).astype(np.float64)
    else:
        nib = np.empty((g, 128, n, 4), np.uint8)
        nib[..., 0::2] = words & 0xF
        nib[..., 1::2] = words >> 4
        vals = E2M1[nib]
    vals = vals * np.repeat(np.exp2(scales.astype(np.float64) - 127.0), 8, axis=1)[..., None]
    return vals.transpose(0, 1, 3, 2).reshape(g * 512, n)


O, K, M, T = 512, 1024, 1536, 1536


def setup_inputs():
    n = np.random.standard_normal
    s = mx_kscale(K)[:, None]
    x = n((K, T)); x[:O] *= 6.0
    w = n((K, M)) / np.sqrt(K) / s; w[:O] /= 2.0
    p_w8 = pack_weight(w[:O], "e4m3")
    p_w4 = pack_weight(w[O:], "e2m1")
    return {
        "x": (x * s).astype(np.float32),
        "w8_words": p_w8[0],
        "w8_scales": p_w8[1],
        "w4_words": p_w4[0],
        "w4_scales": p_w4[1],
        "g": (n((1536, 1536))).astype(np.float32),
    }


def reference(x, w8_words, w8_scales, w4_words, w4_scales, g):
    x_ = mxq(f64(x), 0, "e4m3")
    w8_ = unpack_weight(w8_words, w8_scales, "e4m3")
    w4_ = unpack_weight(w4_words, w4_scales, "e2m1")
    y = x_[:O].T @ w8_ + x_[O:].T @ w4_
    return f64(g) * y

@@ -1,0 +1,130 @@
+from contextlib import ExitStack
+
+import concourse.mybir as mybir
+
+K, T, N = 1024, 1536, 1536
+FLOPS = 2 * K * T * N
+
+F32 = mybir.dt.float32
+BF16 = mybir.dt.bfloat16
+I32 = mybir.dt.int32
+U32 = mybir.dt.uint32
+U8 = mybir.dt.uint8
+E4M3_X4 = mybir.dt.float8_e4m3fn_x4
+E2M1_X4 = mybir.dt.float4_e2m1fn_x4
+MULT = mybir.AluOpType.mult
+
+P = 128
+PACK = 4
+K_PASS = P * PACK
+PASSES = K // K_PASS
+ROWS = 4
+T_CHUNK = P * ROWS
+CHUNKS = T // T_CHUNK
+N_TILE = 512
+N_TILES = N // N_TILE
+
+
+def tile_mix_outl_tm_mul_kernel(tc, x, w8_words, w8_scales, w4_words, w4_scales, g, out):
+    nc = tc.nc
+    with ExitStack() as ctx:
+        keep = ctx.enter_context(tc.tile_pool(name="keep", bufs=1))
+        stage = ctx.enter_context(tc.tile_pool(name="stage", bufs=3))
+        psum = ctx.enter_context(tc.psum_pool(name="psum", bufs=8))
+        ctx.enter_context(tc.manual_schedule())
+
+        planes = []
+        for a in range(PASSES):
+            plane = keep.tile([P, N], U8, name=f"plane{a}", align_bytes=64)
+            nc.vector.memset(plane[:].bitcast(I32), 0)
+            planes.append(plane)
+
+        x_raw = []
+        for a in range(PASSES):
+            raw = keep.tile([P, PACK, T], F32, name=f"x_raw{a}")
+            x_raw.append(raw)
+        x_rows = [x[a * K_PASS : (a + 1) * K_PASS, :].rearrange("(p j) t -> p j t", j=PACK) for a in range(PASSES)]
+        w8 = keep.tile([P, N], U32, name="w8", align_bytes=64)
+        w4 = keep.tile([P, 2 * N], U8, name="w4", align_bytes=64)
+
+        def load_scale_rows(plane, scales, quadrants):
+            for q in quadrants:
+                nc.sync.dma_start(
+                    out=plane[32 * q : 32 * q + 4, :].bitcast(I32),
+                    in_=scales[0, 4 * q : 4 * q + 4, :].bitcast(I32),
+                )
+
+        nc.sync.dma_start(out=x_raw[0][:], in_=x_rows[0])
+        load_scale_rows(planes[0], w8_scales, range(0, 3))
+        nc.sync.dma_start(out=x_raw[1][:], in_=x_rows[1])
+        load_scale_rows(planes[0], w8_scales, range(3, 4))
+        load_scale_rows(planes[1], w4_scales, range(0, 2))
+        nc.sync.dma_start(out=w8[:].bitcast(I32), in_=w8_words[0].rearrange("p n i -> p (n i)").bitcast(I32))
+        load_scale_rows(planes[1], w4_scales, range(2, 4))
+        nc.sync.dma_start(out=w4[:].bitcast(I32), in_=w4_words[0].bitcast(I32))
+
+        g_tiles = []
+        for c in range(CHUNKS):
+            gt = keep.tile([P, ROWS, N], F32, name=f"g{c}")
+            rows = g[c * T_CHUNK : (c + 1) * T_CHUNK, :].rearrange("(m i) n -> m i n", i=ROWS)
+            nc.sync.dma_start(out=gt[:], in_=rows)
+            g_tiles.append(gt)
+
+        def cast(engine_copy, a, c):
+            grouped = stage.tile([P, ROWS, P, PACK], BF16, name=f"grouped{a}", align_bytes=64)
+            src = x_raw[a][:, :, c * T_CHUNK : (c + 1) * T_CHUNK].rearrange("p j (m i) -> p i m j", i=ROWS)
+            engine_copy(out=grouped[:], in_=src)
+            return grouped
+
+        def quantize(grouped, a, c):
+            codes = keep.tile([P, T_CHUNK], U32, name=f"codes{a}_{c}", align_bytes=64)
+            scales = keep.tile([P, T_CHUNK], U8, name=f"scales{a}_{c}", align_bytes=64)
+            nc.vector.quantize_mx(
+                out=codes[:].bitcast(E4M3_X4),
+                scales=scales[:],
+                in_=grouped[:].rearrange("p i m j -> p (i m j)"),
+            )
+            return codes, scales
+
+        vcopy, scopy = nc.vector.tensor_copy, nc.scalar.copy
+        grouped = {}
+        xq = {}
+        grouped[0, 0] = cast(vcopy, 0, 0)
+        grouped[0, 1] = cast(scopy, 0, 1)
+        grouped[0, 2] = cast(vcopy, 0, 2)
+        xq[0, 0] = quantize(grouped[0, 0], 0, 0)
+        xq[0, 1] = quantize(grouped[0, 1], 0, 1)
+        xq[0, 2] = quantize(grouped[0, 2], 0, 2)
+        grouped[1, 0] = cast(vcopy, 1, 0)
+        grouped[1, 1] = cast(scopy, 1, 1)
+        grouped[1, 2] = cast(scopy, 1, 2)
+        for c in range(CHUNKS):
+            xq[1, c] = quantize(grouped[1, c], 1, c)
+
+        def rhs(a, n0):
+            if a == 0:
+                return w8[:, n0 : n0 + N_TILE].bitcast(E4M3_X4)
+            return w4[:, 2 * n0 : 2 * (n0 + N_TILE)].bitcast(E2M1_X4)
+
+        for c in range(CHUNKS):
+            for i in range(ROWS):
+                cols = slice(i * P, (i + 1) * P)
+                accs = [psum.tile([P, N_TILE], F32, name="acc") for b in range(N_TILES)]
+                for a in range(PASSES):
+                    codes, scales = xq[a, c]
+                    for b in range(N_TILES):
+                        n0 = b * N_TILE
+                        nc.tensor.matmul_mx(
+                            out=accs[b][:],
+                            lhsT=codes[:, cols].bitcast(E4M3_X4),
+                            lhsT_scale=scales[:, cols],
+                            rhs=rhs(a, n0),
+                            rhs_scale=planes[a][:, n0 : n0 + N_TILE],
+                            start=(a == 0),
+                            stop=(a == PASSES - 1),
+                        )
+                for b in range(N_TILES):
+                    part = g_tiles[c][:, i, b * N_TILE : (b + 1) * N_TILE]
+                    nc.vector.tensor_tensor(out=part, in0=accs[b][:], in1=part, op=MULT)
+            rows = out[c * T_CHUNK : (c + 1) * T_CHUNK, :].rearrange("(m i) n -> m i n", i=ROWS)
+            nc.sync.dma_start(out=rows, in_=g_tiles[c][:])

@@ -47,28 +47,33 @@ def tile_mix_outl_tm_mul_kernel(tc, x, w8_words, w8_scales, w4_words, w4_scales,
         w8 = keep.tile([P, N], U32, name="w8", align_bytes=64)
         w4 = keep.tile([P, 2 * N], U8, name="w4", align_bytes=64)
 
-        def load_scale_rows(plane, scales, quadrants):
-            for q in quadrants:
+        def load_scale_rows(plane, scales, rests):
+            for r in rests:
                 nc.sync.dma_start(
-                    out=plane[32 * q : 32 * q + 4, :].bitcast(I32),
-                    in_=scales[0, 4 * q : 4 * q + 4, :].bitcast(I32),
+                    out=plane[r:P:32, :].bitcast(I32),
+                    in_=scales[0, r:16:4, :].bitcast(I32),
                 )
+
+        g_tiles = []
+        for c in range(CHUNKS):
+            gt = keep.tile([P, ROWS, N], F32, name=f"g{c}")
+            g_tiles.append(gt)
+
+        def load_g(c):
+            rows = g[c * T_CHUNK : (c + 1) * T_CHUNK, :].rearrange("(m i) n -> m i n", i=ROWS)
+            nc.sync.dma_start(out=g_tiles[c][:], in_=rows)
 
         nc.sync.dma_start(out=x_raw[0][:], in_=x_rows[0])
         load_scale_rows(planes[0], w8_scales, range(0, 3))
         nc.sync.dma_start(out=x_raw[1][:], in_=x_rows[1])
         load_scale_rows(planes[0], w8_scales, range(3, 4))
         load_scale_rows(planes[1], w4_scales, range(0, 2))
-        nc.sync.dma_start(out=w8[:].bitcast(I32), in_=w8_words[0].rearrange("p n i -> p (n i)").bitcast(I32))
+        load_g(0)
         load_scale_rows(planes[1], w4_scales, range(2, 4))
+        nc.sync.dma_start(out=w8[:].bitcast(I32), in_=w8_words[0].rearrange("p n i -> p (n i)").bitcast(I32))
         nc.sync.dma_start(out=w4[:].bitcast(I32), in_=w4_words[0].bitcast(I32))
-
-        g_tiles = []
-        for c in range(CHUNKS):
-            gt = keep.tile([P, ROWS, N], F32, name=f"g{c}")
-            rows = g[c * T_CHUNK : (c + 1) * T_CHUNK, :].rearrange("(m i) n -> m i n", i=ROWS)
-            nc.sync.dma_start(out=gt[:], in_=rows)
-            g_tiles.append(gt)
+        load_g(1)
+        load_g(2)
 
         def cast(engine_copy, a, c):
             grouped = stage.tile([P, ROWS, P, PACK], BF16, name=f"grouped{a}", align_bytes=64)

from contextlib import ExitStack

import concourse.mybir as mybir

K, T, N = 1024, 1536, 1536
FLOPS = 2 * K * T * N

F32 = mybir.dt.float32
BF16 = mybir.dt.bfloat16
I32 = mybir.dt.int32
U32 = mybir.dt.uint32
U8 = mybir.dt.uint8
E4M3_X4 = mybir.dt.float8_e4m3fn_x4
E2M1_X4 = mybir.dt.float4_e2m1fn_x4
MULT = mybir.AluOpType.mult

P = 128
PACK = 4
K_PASS = P * PACK
PASSES = K // K_PASS
ROWS = 4
T_CHUNK = P * ROWS
CHUNKS = T // T_CHUNK
N_TILE = 512
N_TILES = N // N_TILE


def tile_mix_outl_tm_mul_kernel(tc, x, w8_words, w8_scales, w4_words, w4_scales, g, out):
    nc = tc.nc
    with ExitStack() as ctx:
        keep = ctx.enter_context(tc.tile_pool(name="keep", bufs=1))
        stage = ctx.enter_context(tc.tile_pool(name="stage", bufs=3))
        psum = ctx.enter_context(tc.psum_pool(name="psum", bufs=8))
        ctx.enter_context(tc.manual_schedule())

        planes = []
        for a in range(PASSES):
            plane = keep.tile([P, N], U8, name=f"plane{a}", align_bytes=64)
            nc.vector.memset(plane[:].bitcast(I32), 0)
            planes.append(plane)

        x_raw = []
        for a in range(PASSES):
            raw = keep.tile([P, PACK, T], F32, name=f"x_raw{a}")
            x_raw.append(raw)
        x_rows = [x[a * K_PASS : (a + 1) * K_PASS, :].rearrange("(p j) t -> p j t", j=PACK) for a in range(PASSES)]
        w8 = keep.tile([P, N], U32, name="w8", align_bytes=64)
        w4 = keep.tile([P, 2 * N], U8, name="w4", align_bytes=64)

        def load_scale_rows(plane, scales, rests):
            for r in rests:
                nc.sync.dma_start(
                    out=plane[r:P:32, :].bitcast(I32),
                    in_=scales[0, r:16:4, :].bitcast(I32),
                )

        g_tiles = []
        for c in range(CHUNKS):
            gt = keep.tile([P, ROWS, N], F32, name=f"g{c}")
            g_tiles.append(gt)

        def load_g(c):
            rows = g[c * T_CHUNK : (c + 1) * T_CHUNK, :].rearrange("(m i) n -> m i n", i=ROWS)
            nc.sync.dma_start(out=g_tiles[c][:], in_=rows)

        nc.sync.dma_start(out=x_raw[0][:], in_=x_rows[0])
        load_scale_rows(planes[0], w8_scales, range(0, 3))
        nc.sync.dma_start(out=x_raw[1][:], in_=x_rows[1])
        load_scale_rows(planes[0], w8_scales, range(3, 4))
        load_scale_rows(planes[1], w4_scales, range(0, 2))
        load_g(0)
        load_scale_rows(planes[1], w4_scales, range(2, 4))
        nc.sync.dma_start(out=w8[:].bitcast(I32), in_=w8_words[0].rearrange("p n i -> p (n i)").bitcast(I32))
        nc.sync.dma_start(out=w4[:].bitcast(I32), in_=w4_words[0].bitcast(I32))
        load_g(1)
        load_g(2)

        def cast(engine_copy, a, c):
            grouped = stage.tile([P, ROWS, P, PACK], BF16, name=f"grouped{a}", align_bytes=64)
            src = x_raw[a][:, :, c * T_CHUNK : (c + 1) * T_CHUNK].rearrange("p j (m i) -> p i m j", i=ROWS)
            engine_copy(out=grouped[:], in_=src)
            return grouped

        def quantize(grouped, a, c):
            codes = keep.tile([P, T_CHUNK], U32, name=f"codes{a}_{c}", align_bytes=64)
            scales = keep.tile([P, T_CHUNK], U8, name=f"scales{a}_{c}", align_bytes=64)
            nc.vector.quantize_mx(
                out=codes[:].bitcast(E4M3_X4),
                scales=scales[:],
                in_=grouped[:].rearrange("p i m j -> p (i m j)"),
            )
            return codes, scales

        vcopy, scopy = nc.vector.tensor_copy, nc.scalar.copy
        grouped = {}
        xq = {}
        grouped[0, 0] = cast(vcopy, 0, 0)
        grouped[0, 1] = cast(scopy, 0, 1)
        grouped[0, 2] = cast(vcopy, 0, 2)
        xq[0, 0] = quantize(grouped[0, 0], 0, 0)
        xq[0, 1] = quantize(grouped[0, 1], 0, 1)
        xq[0, 2] = quantize(grouped[0, 2], 0, 2)
        grouped[1, 0] = cast(vcopy, 1, 0)
        grouped[1, 1] = cast(scopy, 1, 1)
        grouped[1, 2] = cast(scopy, 1, 2)
        for c in range(CHUNKS):
            xq[1, c] = quantize(grouped[1, c], 1, c)

        def rhs(a, n0):
            if a == 0:
                return w8[:, n0 : n0 + N_TILE].bitcast(E4M3_X4)
            return w4[:, 2 * n0 : 2 * (n0 + N_TILE)].bitcast(E2M1_X4)

        for c in range(CHUNKS):
            for i in range(ROWS):
                cols = slice(i * P, (i + 1) * P)
                accs = [psum.tile([P, N_TILE], F32, name="acc") for b in range(N_TILES)]
                for a in range(PASSES):
                    codes, scales = xq[a, c]
                    for b in range(N_TILES):
                        n0 = b * N_TILE
                        nc.tensor.matmul_mx(
                            out=accs[b][:],
                            lhsT=codes[:, cols].bitcast(E4M3_X4),
                            lhsT_scale=scales[:, cols],
                            rhs=rhs(a, n0),
                            rhs_scale=planes[a][:, n0 : n0 + N_TILE],
                            start=(a == 0),
                            stop=(a == PASSES - 1),
                        )
                for b in range(N_TILES):
                    part = g_tiles[c][:, i, b * N_TILE : (b + 1) * N_TILE]
                    nc.vector.tensor_tensor(out=part, in0=accs[b][:], in1=part, op=MULT)
            rows = out[c * T_CHUNK : (c + 1) * T_CHUNK, :].rearrange("(m i) n -> m i n", i=ROWS)
            nc.sync.dma_start(out=rows, in_=g_tiles[c][:])
